import numpy as np, ml_dtypes
CORES = [23,39,55,63,87,103,111,127,18,34,50,58,82,98,106,122]
N = 16
VB, TK = 1, 128
def setup_inputs(rng):
    h = (rng.standard_normal((128, TK), dtype=np.float32) / 8).astype(ml_dtypes.bfloat16)
    return {"h": np.broadcast_to(h, (N, 128, TK)).copy(), "w": rng.standard_normal((N, 128, VB * 128), dtype=np.float32).astype(ml_dtypes.bfloat16)}
def setup_inputs_big(rng):
    d = setup_inputs(rng)
    for k in ("h", "w"): d[k] = (d[k].astype(np.float32) * 1024.0).astype(d[k].dtype)
    return d
def setup_inputs_small(rng):
    d = setup_inputs(rng)
    for k in ("h", "w"): d[k] = (d[k].astype(np.float32) * (1 / 1024.0)).astype(d[k].dtype)
    return d
def setup_inputs_apart(rng):
    d = setup_inputs(rng)
    f = (10.0 ** rng.permutation(np.linspace(-1.5, 1.5, N))).astype(np.float32).reshape(N, 1, 1)
    for k in ("w",): d[k] = (d[k].astype(np.float32) * f).astype(d[k].dtype)
    return d
def setup_inputs_neg(rng):
    d = setup_inputs(rng)
    d["h"] = (np.abs(d["h"].astype(np.float32)) * 1048576.0).astype(d["h"].dtype); d["w"] = (-np.abs(d["w"].astype(np.float32))).astype(d["w"].dtype)
    return d
def reference(h, w):
    H, W = h.astype(np.float64), w.astype(np.float64)
    Z = np.concatenate([W[r].T @ H[r] for r in range(N)], axis=0)
    m = Z.max(axis=0)
    s = np.maximum(Z - 0.5 * m, 0.0).sum(axis=0)
    return {"m": np.broadcast_to(m.astype(np.float32), (N, 1, TK)), "s": np.broadcast_to(s.astype(np.float32), (N, 1, TK))}

@@ -1,0 +1,180 @@
+from concourse.bass import DstId, RemoteDMATransfer
+from concourse.mybir import AluOpType
+
+N = 16
+COL_ENGINES = 8
+
+SCRATCH = {
+    "h_sb": ("sbuf", [128, 128], "bfloat16"),
+    "w_sb": ("sbuf", [128, 128], "bfloat16"),
+    "zt_ps": ("psum", [128, 512], "float32"),
+    "z_ps": ("psum", [128, 512], "float32"),
+    "s_ps": ("psum", [128, 512], "float32"),
+    "tr": ("sbuf", [128, 256], "float32"),
+    "mcol": ("sbuf", [128, 4], "float32"),
+    "scol": ("sbuf", [128, 4], "float32"),
+    "nh": ("sbuf", [128, 128], "float32"),
+    "zero": ("sbuf", [128, 128], "float32"),
+    "one": ("sbuf", [128, 4], "float32"),
+    "mrow": ("sbuf", [128, 128], "float32"),
+    "relu": ("sbuf", [128, 128], "float32"),
+    "mslot": ("dram", [N, 128, 1], "float32"),
+    "sslot": ("dram", [N, 128, 1], "float32"),
+    "mres": ("dram", [128, 1], "float32"),
+    "sres": ("dram", [128, 1], "float32"),
+}
+SEMAPHORES = ["ld", "fill", "mm", "v", "arra", "arrb", "gotm", "gots", "mld", "out", "sent"]
+
+
+def _hops(topo, a, b):
+    ca, cb = topo.chip(a), topo.chip(b)
+    if ca == cb:
+        return 0
+    if topo.mates(ca, cb) or topo.same_plane(ca, cb):
+        return 1
+    return 2
+
+
+def _plan(cores, topo):
+    best = None
+    for x in cores:
+        for y in cores:
+            if x == y or not (topo.may_write(x, y) and topo.may_write(y, x)):
+                continue
+            if not all(topo.may_write(c, hb) for hb in (x, y) for c in cores if c != hb):
+                continue
+            serve = {x: [y], y: [x]}
+            ok = True
+            for c in cores:
+                if c == x or c == y:
+                    continue
+                cand = [hb for hb in (x, y) if topo.may_write(hb, c)]
+                if not cand:
+                    ok = False
+                    break
+                hb = min(cand, key=lambda q: (_hops(topo, q, c), len(serve[q])))
+                serve[hb].append(c)
+            if not ok:
+                continue
+            score = sum(_hops(topo, hb, c) for hb in (x, y) for c in serve[hb])
+            if best is None or score < best[0]:
+                best = (score, x, y, serve)
+    return best[1], best[2], best[3]
+
+
+def _engines(topo, src, dsts, n):
+    m = topo.mask(src, dsts[0])
+    for d in dsts[1:]:
+        m &= topo.mask(src, d)
+    bits = [1 << b for b in range(m.bit_length()) if (m >> b) & 1]
+    k = 1
+    while k * 2 <= min(n, len(bits)):
+        k *= 2
+    return bits[:k]
+
+
+def _dst(topo, c):
+    rid, pid, _ = topo.addr(c)
+    return DstId(rid=rid, pnc=pid)
+
+
+def rank_program(g, core, T, topo):
+    rank = T.rank_of(core)
+    if rank is None:
+        return
+    S = T.sem
+    cores = list(T.cores)
+    hub_x, hub_y, serve = _plan(cores, topo)
+    hubs = (hub_x, hub_y)
+    is_hub = core in hubs
+    sent = [0]
+    nv = [0]
+
+    def vdone(inst):
+        inst.then_inc(S.v, 1)
+        nv[0] += 1
+
+    def col_width(src):
+        return len(_engines(topo, src, [hb for hb in hubs if hb != src], COL_ENGINES))
+
+    def send_col(col, slots, arr):
+        dsts = [hb for hb in hubs if hb != core]
+        eng = _engines(topo, core, dsts, COL_ENGINES)
+        g.remote_dma_fused([RemoteDMATransfer(
+            dst_ids=[_dst(topo, d) for d in dsts], dma_engine_mask=sum(eng), remote_sem=arr,
+            srcs=[col], dsts=[slots[rank] for _ in dsts], alu_op=0)], local_sem=S.sent)
+        sent[0] += len(eng)
+
+    def fold(slots, res, arr, got, op):
+        g.wait_ge(arr, 16 + sum(col_width(c) for c in cores if c != core))
+        mine = serve[core]
+        eng = _engines(topo, core, mine, min(COL_ENGINES, len(mine)))
+        trs = []
+        for j, e in enumerate(eng):
+            part = mine[j::len(eng)]
+            trs.append(RemoteDMATransfer(
+                dst_ids=[_dst(topo, d) for d in part], dma_engine_mask=e, remote_sem=got,
+                srcs=[slots[k] for k in range(N)], dsts=[res[:] for _ in part], alu_op=op))
+        g.remote_dma_fused(trs, local_sem=S.sent)
+        sent[0] += len(eng)
+
+    g.vector.memset(T.nh[0:1, :], -0.5).then_inc(S.fill, 1)
+    g.vector.memset(T.zero[:], 0.0).then_inc(S.fill, 1)
+    g.vector.memset(T.one[:], 1.0).then_inc(S.fill, 1)
+
+    g.sync.dma_start(T.h_sb[:], T.h[:]).then_inc(S.ld, 16)
+    g.scalar.dma_start(T.w_sb[:], T.w[:]).then_inc(S.ld, 16)
+
+    g.tensor.wait_ge(S.ld, 32)
+    g.tensor.matmul(T.zt_ps[:, 0:128], T.h_sb[:], T.w_sb[:], True, True).then_inc(S.mm, 1)
+    g.tensor.matmul(T.z_ps[:, 0:128], T.w_sb[:], T.h_sb[:], True, False)
+
+    tr = T.tr
+    g.vector.wait_ge(S.mm, 1)
+    vdone(g.vector.tensor_copy(tr[:, 0:64], T.zt_ps[:, 64:128]))
+    g.vector.wait_ge(S.v, nv[0])
+    vdone(g.vector.tensor_tensor(tr[:, 64:128], T.zt_ps[:, 0:64], tr[:, 0:64], AluOpType.max))
+    off, wd = 64, 64
+    while wd > 1:
+        half = wd // 2
+        out = tr[:, off + wd:off + wd + half] if half > 1 else T.mcol[:, 0:1]
+        g.vector.wait_ge(S.v, nv[0])
+        vdone(g.vector.tensor_tensor(out, tr[:, off:off + half], tr[:, off + half:off + wd], AluOpType.max))
+        off, wd = off + wd, half
+    n_max = nv[0]
+
+    g.wait_ge(S.v, n_max)
+    send_col(T.mcol[:, 0:1], T.mslot, S.arra)
+    if is_hub:
+        g.sync.wait_ge(S.v, n_max)
+        g.sync.dma_start(T.mslot[rank], T.mcol[:, 0:1]).then_inc(S.arra, 16)
+        fold(T.mslot, T.mres, S.arra, S.gotm, 2)
+
+    g.sync.wait_ge(S.gotm, 1)
+    g.sync.dma_start(T.mrow[0:1, :], T.mres[:]).then_inc(S.mld, 16)
+    g.scalar.wait_ge(S.gotm, 1)
+    g.scalar.dma_start(T.m[:], T.mres[:]).then_inc(S.out, 16)
+
+    g.tensor.wait_ge(S.fill, 3)
+    g.tensor.wait_ge(S.mld, 16)
+    g.tensor.matmul(T.z_ps[:, 0:128], T.nh[0:1, :], T.mrow[0:1, :], False, True).then_inc(S.mm, 1)
+    g.vector.wait_ge(S.fill, 3)
+    g.vector.wait_ge(S.mm, 2)
+    vdone(g.vector.tensor_tensor(T.relu[:], T.z_ps[:, 0:128], T.zero[:], AluOpType.max))
+    g.tensor.wait_ge(S.v, nv[0])
+    g.tensor.matmul(T.s_ps[:, 0:1], T.relu[:], T.one[:, 0:1], True, True).then_inc(S.mm, 1)
+    g.vector.wait_ge(S.mm, 3)
+    vdone(g.vector.tensor_copy(T.scol[:, 0:1], T.s_ps[:, 0:1]))
+    n_sum = nv[0]
+
+    g.wait_ge(S.v, n_sum)
+    send_col(T.scol[:, 0:1], T.sslot, S.arrb)
+    if is_hub:
+        g.sync.wait_ge(S.v, n_sum)
+        g.sync.dma_start(T.sslot[rank], T.scol[:, 0:1]).then_inc(S.arrb, 16)
+        fold(T.sslot, T.sres, S.arrb, S.gots, 1)
+
+    g.sync.wait_ge(S.gots, 1)
+    g.sync.dma_start(T.s[:], T.sres[:]).then_inc(S.out, 16)
+    g.sync.wait_ge(S.out, 32)
+    g.wait_ge(S.sent, sent[0])

@@ -1,29 +1,30 @@
 from concourse.bass import DstId, RemoteDMATransfer
-from concourse.mybir import AluOpType
+from concourse.mybir import AluOpType, AxisListType, ActivationFunctionType
 
 N = 16
-COL_ENGINES = 8
+SEND_ENGINES = 2
 
 SCRATCH = {
     "h_sb": ("sbuf", [128, 128], "bfloat16"),
     "w_sb": ("sbuf", [128, 128], "bfloat16"),
     "zt_ps": ("psum", [128, 512], "float32"),
-    "z_ps": ("psum", [128, 512], "float32"),
+    "mt_ps": ("psum", [128, 512], "float32"),
     "s_ps": ("psum", [128, 512], "float32"),
-    "tr": ("sbuf", [128, 256], "float32"),
     "mcol": ("sbuf", [128, 4], "float32"),
+    "negm": ("sbuf", [128, 4], "float32"),
+    "gm": ("sbuf", [128, 4], "float32"),
     "scol": ("sbuf", [128, 4], "float32"),
-    "nh": ("sbuf", [128, 128], "float32"),
-    "zero": ("sbuf", [128, 128], "float32"),
-    "one": ("sbuf", [128, 4], "float32"),
-    "mrow": ("sbuf", [128, 128], "float32"),
+    "sfin": ("sbuf", [128, 4], "float32"),
     "relu": ("sbuf", [128, 128], "float32"),
-    "mslot": ("dram", [N, 128, 1], "float32"),
-    "sslot": ("dram", [N, 128, 1], "float32"),
-    "mres": ("dram", [128, 1], "float32"),
-    "sres": ("dram", [128, 1], "float32"),
+    "ones16": ("sbuf", [128, 16], "float32"),
+    "ident": ("sbuf", [128, 16], "float32"),
+    "half": ("sbuf", [128, 4], "float32"),
+    "mall_sb": ("sbuf", [128, 128], "float32"),
+    "sall_sb": ("sbuf", [128, 128], "float32"),
+    "mall": ("dram", [N, 128, 1], "float32"),
+    "sall": ("dram", [N, 128, 1], "float32"),
 }
-SEMAPHORES = ["ld", "fill", "mm", "v", "arra", "arrb", "gotm", "gots", "mld", "out", "sent"]
+SEMAPHORES = ["ld", "fill", "idn", "mm", "v", "vm", "sc", "la", "lb", "lma", "lsb", "arra", "arrb", "out", "sent"]
 
 
 def _hops(topo, a, b):
@@ -35,42 +36,12 @@ def _hops(topo, a, b):
     return 2
 
 
-def _plan(cores, topo):
-    best = None
-    for x in cores:
-        for y in cores:
-            if x == y or not (topo.may_write(x, y) and topo.may_write(y, x)):
-                continue
-            if not all(topo.may_write(c, hb) for hb in (x, y) for c in cores if c != hb):
-                continue
-            serve = {x: [y], y: [x]}
-            ok = True
-            for c in cores:
-                if c == x or c == y:
-                    continue
-                cand = [hb for hb in (x, y) if topo.may_write(hb, c)]
-                if not cand:
-                    ok = False
-                    break
-                hb = min(cand, key=lambda q: (_hops(topo, q, c), len(serve[q])))
-                serve[hb].append(c)
-            if not ok:
-                continue
-            score = sum(_hops(topo, hb, c) for hb in (x, y) for c in serve[hb])
-            if best is None or score < best[0]:
-                best = (score, x, y, serve)
-    return best[1], best[2], best[3]
-
-
 def _engines(topo, src, dsts, n):
     m = topo.mask(src, dsts[0])
     for d in dsts[1:]:
         m &= topo.mask(src, d)
     bits = [1 << b for b in range(m.bit_length()) if (m >> b) & 1]
-    k = 1
-    while k * 2 <= min(n, len(bits)):
-        k *= 2
-    return bits[:k]
+    return bits[:n]
 
 
 def _dst(topo, c):
@@ -83,98 +54,67 @@ def rank_program(g, core, T, topo):
     if rank is None:
         return
     S = T.sem
-    cores = list(T.cores)
-    hub_x, hub_y, serve = _plan(cores, topo)
-    hubs = (hub_x, hub_y)
-    is_hub = core in hubs
-    sent = [0]
-    nv = [0]
+    others = [c for c in T.cores if c != core]
+    assert all(topo.may_write(core, c) for c in others)
+    others.sort(key=lambda c: -_hops(topo, core, c))
+    eng = _engines(topo, core, others, SEND_ENGINES)
 
-    def vdone(inst):
-        inst.then_inc(S.v, 1)
-        nv[0] += 1
-
-    def col_width(src):
-        return len(_engines(topo, src, [hb for hb in hubs if hb != src], COL_ENGINES))
-
-    def send_col(col, slots, arr):
-        dsts = [hb for hb in hubs if hb != core]
-        eng = _engines(topo, core, dsts, COL_ENGINES)
-        g.remote_dma_fused([RemoteDMATransfer(
-            dst_ids=[_dst(topo, d) for d in dsts], dma_engine_mask=sum(eng), remote_sem=arr,
-            srcs=[col], dsts=[slots[rank] for _ in dsts], alu_op=0)], local_sem=S.sent)
-        sent[0] += len(eng)
-
-    def fold(slots, res, arr, got, op):
-        g.wait_ge(arr, 16 + sum(col_width(c) for c in cores if c != core))
-        mine = serve[core]
-        eng = _engines(topo, core, mine, min(COL_ENGINES, len(mine)))
+    def spread(table, arr):
         trs = []
         for j, e in enumerate(eng):
-            part = mine[j::len(eng)]
+            part = others[j::len(eng)]
             trs.append(RemoteDMATransfer(
-                dst_ids=[_dst(topo, d) for d in part], dma_engine_mask=e, remote_sem=got,
-                srcs=[slots[k] for k in range(N)], dsts=[res[:] for _ in part], alu_op=op))
+                dst_ids=[_dst(topo, d) for d in part], dma_engine_mask=e, remote_sem=arr,
+                srcs=[table[rank]], dsts=[table[rank] for _ in part], alu_op=0))
         g.remote_dma_fused(trs, local_sem=S.sent)
-        sent[0] += len(eng)
-
-    g.vector.memset(T.nh[0:1, :], -0.5).then_inc(S.fill, 1)
-    g.vector.memset(T.zero[:], 0.0).then_inc(S.fill, 1)
-    g.vector.memset(T.one[:], 1.0).then_inc(S.fill, 1)
 
     g.sync.dma_start(T.h_sb[:], T.h[:]).then_inc(S.ld, 16)
     g.scalar.dma_start(T.w_sb[:], T.w[:]).then_inc(S.ld, 16)
 
+    g.vector.memset(T.ones16[0:16, :], 1.0).then_inc(S.fill, 1)
+    g.vector.memset(T.half[0:16, :], 0.5).then_inc(S.fill, 1)
+    g.wait_ge(S.fill, 2)
+    g.affine_select(T.ident[0:16, :], T.ones16[0:16, :], [[-1, 16]], AluOpType.is_equal, 0.0, 0, 1).then_inc(S.idn, 1)
+
     g.tensor.wait_ge(S.ld, 32)
     g.tensor.matmul(T.zt_ps[:, 0:128], T.h_sb[:], T.w_sb[:], True, True).then_inc(S.mm, 1)
-    g.tensor.matmul(T.z_ps[:, 0:128], T.w_sb[:], T.h_sb[:], True, False)
-
-    tr = T.tr
     g.vector.wait_ge(S.mm, 1)
-    vdone(g.vector.tensor_copy(tr[:, 0:64], T.zt_ps[:, 64:128]))
-    g.vector.wait_ge(S.v, nv[0])
-    vdone(g.vector.tensor_tensor(tr[:, 64:128], T.zt_ps[:, 0:64], tr[:, 0:64], AluOpType.max))
-    off, wd = 64, 64
-    while wd > 1:
-        half = wd // 2
-        out = tr[:, off + wd:off + wd + half] if half > 1 else T.mcol[:, 0:1]
-        g.vector.wait_ge(S.v, nv[0])
-        vdone(g.vector.tensor_tensor(out, tr[:, off:off + half], tr[:, off + half:off + wd], AluOpType.max))
-        off, wd = off + wd, half
-    n_max = nv[0]
+    g.vector.tensor_reduce(T.mcol[:, 0:1], T.zt_ps[:, 0:128], AxisListType.X, AluOpType.max).then_inc(S.v, 1)
 
-    g.wait_ge(S.v, n_max)
-    send_col(T.mcol[:, 0:1], T.mslot, S.arra)
-    if is_hub:
-        g.sync.wait_ge(S.v, n_max)
-        g.sync.dma_start(T.mslot[rank], T.mcol[:, 0:1]).then_inc(S.arra, 16)
-        fold(T.mslot, T.mres, S.arra, S.gotm, 2)
-
-    g.sync.wait_ge(S.gotm, 1)
-    g.sync.dma_start(T.mrow[0:1, :], T.mres[:]).then_inc(S.mld, 16)
-    g.scalar.wait_ge(S.gotm, 1)
-    g.scalar.dma_start(T.m[:], T.mres[:]).then_inc(S.out, 16)
-
-    g.tensor.wait_ge(S.fill, 3)
-    g.tensor.wait_ge(S.mld, 16)
-    g.tensor.matmul(T.z_ps[:, 0:128], T.nh[0:1, :], T.mrow[0:1, :], False, True).then_inc(S.mm, 1)
-    g.vector.wait_ge(S.fill, 3)
+    g.sync.wait_ge(S.v, 1)
+    g.sync.dma_start(T.mall[rank], T.mcol[:, 0:1]).then_inc(S.la, 16)
+    g.wait_ge(S.la, 16)
+    spread(T.mall, S.arra)
+    g.sync.wait_ge(S.la, 16)
+    g.sync.wait_ge(S.arra, N - 1)
+    g.sync.dma_start(T.mall_sb[0:16, :], T.mall[:]).then_inc(S.lma, 16)
+    g.tensor.wait_ge(S.idn, 1)
+    g.tensor.wait_ge(S.lma, 16)
+    g.tensor.matmul(T.mt_ps[:, 0:16], T.mall_sb[0:16, :], T.ident[0:16, :], True, True).then_inc(S.mm, 1)
     g.vector.wait_ge(S.mm, 2)
-    vdone(g.vector.tensor_tensor(T.relu[:], T.z_ps[:, 0:128], T.zero[:], AluOpType.max))
-    g.tensor.wait_ge(S.v, nv[0])
-    g.tensor.matmul(T.s_ps[:, 0:1], T.relu[:], T.one[:, 0:1], True, True).then_inc(S.mm, 1)
+    g.vector.tensor_reduce(T.negm[:, 0:1], T.mt_ps[:, 0:16], AxisListType.X, AluOpType.max,
+                           negate=True).then_inc(S.v, 1)
+    g.vector.tensor_reduce(T.gm[:, 0:1], T.mt_ps[:, 0:16], AxisListType.X, AluOpType.max).then_inc(S.vm, 1)
+
+    g.scalar.wait_ge(S.v, 2)
+    g.scalar.activation(T.relu[:], T.zt_ps[:, 0:128], ActivationFunctionType.Relu, bias=T.negm[:, 0:1], scale=2.0,
+                        accum_out=T.scol[:, 0:1]).then_inc(S.sc, 1)
+    g.scalar.wait_ge(S.vm, 1)
+    g.scalar.dma_start(T.m[:], T.gm[:, 0:1]).then_inc(S.out, 16)
+
+    g.sync.wait_ge(S.sc, 1)
+    g.sync.dma_start(T.sall[rank], T.scol[:, 0:1]).then_inc(S.lb, 16)
+    g.wait_ge(S.lb, 16)
+    spread(T.sall, S.arrb)
+    g.sync.wait_ge(S.lb, 16)
+    g.sync.wait_ge(S.arrb, N - 1)
+    g.sync.dma_start(T.sall_sb[0:16, :], T.sall[:]).then_inc(S.lsb, 16)
+    g.tensor.wait_ge(S.fill, 2)
+    g.tensor.wait_ge(S.lsb, 16)
+    g.tensor.matmul(T.s_ps[:, 0:1], T.sall_sb[0:16, :], T.half[0:16, 0:1], True, True).then_inc(S.mm, 1)
     g.vector.wait_ge(S.mm, 3)
-    vdone(g.vector.tensor_copy(T.scol[:, 0:1], T.s_ps[:, 0:1]))
-    n_sum = nv[0]
-
-    g.wait_ge(S.v, n_sum)
-    send_col(T.scol[:, 0:1], T.sslot, S.arrb)
-    if is_hub:
-        g.sync.wait_ge(S.v, n_sum)
-        g.sync.dma_start(T.sslot[rank], T.scol[:, 0:1]).then_inc(S.arrb, 16)
-        fold(T.sslot, T.sres, S.arrb, S.gots, 1)
-
-    g.sync.wait_ge(S.gots, 1)
-    g.sync.dma_start(T.s[:], T.sres[:]).then_inc(S.out, 16)
+    g.vector.tensor_copy(T.sfin[:, 0:1], T.s_ps[:, 0:1]).then_inc(S.v, 1)
+    g.sync.wait_ge(S.v, 3)
+    g.sync.dma_start(T.s[:], T.sfin[:, 0:1]).then_inc(S.out, 16)
     g.sync.wait_ge(S.out, 32)
-    g.wait_ge(S.sent, sent[0])
+    g.wait_ge(S.sent, 2 * len(eng))

@@ -2,29 +2,28 @@ from concourse.bass import DstId, RemoteDMATransfer
 from concourse.mybir import AluOpType, AxisListType, ActivationFunctionType
 
 N = 16
-SEND_ENGINES = 2
+ENGINES = 4
 
 SCRATCH = {
     "h_sb": ("sbuf", [128, 128], "bfloat16"),
     "w_sb": ("sbuf", [128, 128], "bfloat16"),
+    "w2_sb": ("sbuf", [128, 128], "bfloat16"),
     "zt_ps": ("psum", [128, 512], "float32"),
     "mt_ps": ("psum", [128, 512], "float32"),
-    "s_ps": ("psum", [128, 512], "float32"),
     "mcol": ("sbuf", [128, 4], "float32"),
-    "negm": ("sbuf", [128, 4], "float32"),
+    "nb": ("sbuf", [128, 4], "float32"),
     "gm": ("sbuf", [128, 4], "float32"),
     "scol": ("sbuf", [128, 4], "float32"),
-    "sfin": ("sbuf", [128, 4], "float32"),
-    "relu": ("sbuf", [128, 128], "float32"),
-    "ones16": ("sbuf", [128, 16], "float32"),
+    "relu": ("sbuf", [128, 256], "float32"),
+    "half16": ("sbuf", [128, 16], "float32"),
     "ident": ("sbuf", [128, 16], "float32"),
-    "half": ("sbuf", [128, 4], "float32"),
     "mall_sb": ("sbuf", [128, 128], "float32"),
-    "sall_sb": ("sbuf", [128, 128], "float32"),
     "mall": ("dram", [N, 128, 1], "float32"),
-    "sall": ("dram", [N, 128, 1], "float32"),
+    "sall": ("dram", [N // 2, 128, 1], "float32"),
+    "sres": ("dram", [128, 1], "float32"),
 }
-SEMAPHORES = ["ld", "fill", "idn", "mm", "v", "vm", "sc", "la", "lb", "lma", "lsb", "arra", "arrb", "out", "sent"]
+SEMAPHORES = ["ldh", "ldw", "fill", "idn", "mm", "v", "vm", "sc", "la", "lb", "lma",
+              "arrw", "arra", "arrb", "gots", "out", "sent"]
 
 
 def _hops(topo, a, b):
@@ -41,7 +40,10 @@ def _engines(topo, src, dsts, n):
     for d in dsts[1:]:
         m &= topo.mask(src, d)
     bits = [1 << b for b in range(m.bit_length()) if (m >> b) & 1]
-    return bits[:n]
+    k = 1
+    while k * 2 <= min(n, len(bits)):
+        k *= 2
+    return bits[:k]
 
 
 def _dst(topo, c):
@@ -54,67 +56,81 @@ def rank_program(g, core, T, topo):
     if rank is None:
         return
     S = T.sem
-    others = [c for c in T.cores if c != core]
+    far_first = lambda c: -_hops(topo, core, c)
+    others = sorted((c for c in T.cores if c != core), key=far_first)
     assert all(topo.may_write(core, c) for c in others)
-    others.sort(key=lambda c: -_hops(topo, core, c))
-    eng = _engines(topo, core, others, SEND_ENGINES)
+    chips = sorted({topo.chip(c) for c in T.cores})
+    on_chip = {ch: sorted((c for c in T.cores if topo.chip(c) == ch), key=topo.die) for ch in chips}
+    assert all(len(v) == 2 for v in on_chip.values())
+    mine = on_chip[topo.chip(core)]
+    mate = mine[1 - mine.index(core)]
+    peers = sorted((on_chip[ch][mine.index(core)] for ch in chips if ch != topo.chip(core)), key=far_first)
+    ci = chips.index(topo.chip(core))
+    nc = len(chips)
+    eng = _engines(topo, core, others, ENGINES)
 
-    def spread(table, arr):
+    def spread(slot, dsts, arr):
         trs = []
         for j, e in enumerate(eng):
-            part = others[j::len(eng)]
+            part = dsts[j::len(eng)]
             trs.append(RemoteDMATransfer(
                 dst_ids=[_dst(topo, d) for d in part], dma_engine_mask=e, remote_sem=arr,
-                srcs=[table[rank]], dsts=[table[rank] for _ in part], alu_op=0))
+                srcs=[slot], dsts=[slot for _ in part], alu_op=0))
         g.remote_dma_fused(trs, local_sem=S.sent)
 
-    g.sync.dma_start(T.h_sb[:], T.h[:]).then_inc(S.ld, 16)
-    g.scalar.dma_start(T.w_sb[:], T.w[:]).then_inc(S.ld, 16)
+    g.scalar.dma_start(T.w_sb[:], T.w[:]).then_inc(S.ldw, 16)
+    g.sync.dma_start(T.h_sb[:], T.h[:]).then_inc(S.ldh, 16)
 
-    g.vector.memset(T.ones16[0:16, :], 1.0).then_inc(S.fill, 1)
-    g.vector.memset(T.half[0:16, :], 0.5).then_inc(S.fill, 1)
-    g.wait_ge(S.fill, 2)
-    g.affine_select(T.ident[0:16, :], T.ones16[0:16, :], [[-1, 16]], AluOpType.is_equal, 0.0, 0, 1).then_inc(S.idn, 1)
+    g.vector.memset(T.half16[0:16, :], 0.5).then_inc(S.fill, 1)
+    g.wait_ge(S.fill, 1)
+    g.affine_select(T.ident[0:16, :], T.half16[0:16, :], [[-1, 16]], AluOpType.is_equal, 0.0, 0, 1).then_inc(S.idn, 1)
 
-    g.tensor.wait_ge(S.ld, 32)
+    g.wait_ge(S.ldw, 16)
+    rid, pid, _ = topo.addr(mate)
+    g.remote_dma(T.w2_sb[:], T.w_sb[:], S.arrw, S.sent, pid, rid, sum(eng))
+
+    g.tensor.wait_ge(S.ldh, 16)
+    g.tensor.wait_ge(S.ldw, 16)
     g.tensor.matmul(T.zt_ps[:, 0:128], T.h_sb[:], T.w_sb[:], True, True).then_inc(S.mm, 1)
     g.vector.wait_ge(S.mm, 1)
     g.vector.tensor_reduce(T.mcol[:, 0:1], T.zt_ps[:, 0:128], AxisListType.X, AluOpType.max).then_inc(S.v, 1)
 
+    g.tensor.wait_ge(S.v, 1)
+    g.tensor.wait_ge(S.arrw, len(eng))
+    g.tensor.matmul(T.zt_ps[:, 128:256], T.h_sb[:], T.w2_sb[:], True, True).then_inc(S.mm, 1)
+
     g.sync.wait_ge(S.v, 1)
     g.sync.dma_start(T.mall[rank], T.mcol[:, 0:1]).then_inc(S.la, 16)
     g.wait_ge(S.la, 16)
-    spread(T.mall, S.arra)
+    spread(T.mall[rank], others, S.arra)
     g.sync.wait_ge(S.la, 16)
-    g.sync.wait_ge(S.arra, N - 1)
+    g.sync.wait_ge(S.arra, len(others))
     g.sync.dma_start(T.mall_sb[0:16, :], T.mall[:]).then_inc(S.lma, 16)
     g.tensor.wait_ge(S.idn, 1)
     g.tensor.wait_ge(S.lma, 16)
     g.tensor.matmul(T.mt_ps[:, 0:16], T.mall_sb[0:16, :], T.ident[0:16, :], True, True).then_inc(S.mm, 1)
-    g.vector.wait_ge(S.mm, 2)
-    g.vector.tensor_reduce(T.negm[:, 0:1], T.mt_ps[:, 0:16], AxisListType.X, AluOpType.max,
+    g.vector.wait_ge(S.mm, 3)
+    g.vector.tensor_reduce(T.nb[:, 0:1], T.mt_ps[:, 0:16], AxisListType.X, AluOpType.max,
                            negate=True).then_inc(S.v, 1)
-    g.vector.tensor_reduce(T.gm[:, 0:1], T.mt_ps[:, 0:16], AxisListType.X, AluOpType.max).then_inc(S.vm, 1)
 
     g.scalar.wait_ge(S.v, 2)
-    g.scalar.activation(T.relu[:], T.zt_ps[:, 0:128], ActivationFunctionType.Relu, bias=T.negm[:, 0:1], scale=2.0,
+    g.scalar.activation(T.relu[:], T.zt_ps[:, 0:256], ActivationFunctionType.Relu, bias=T.nb[:, 0:1], scale=1.0,
                         accum_out=T.scol[:, 0:1]).then_inc(S.sc, 1)
+
+    g.vector.wait_ge(S.v, 2)
+    g.vector.tensor_scalar(T.gm[:, 0:1], T.nb[:, 0:1], -2.0, None, AluOpType.mult).then_inc(S.vm, 1)
     g.scalar.wait_ge(S.vm, 1)
     g.scalar.dma_start(T.m[:], T.gm[:, 0:1]).then_inc(S.out, 16)
 
     g.sync.wait_ge(S.sc, 1)
-    g.sync.dma_start(T.sall[rank], T.scol[:, 0:1]).then_inc(S.lb, 16)
+    g.sync.dma_start(T.sall[ci], T.scol[:, 0:1]).then_inc(S.lb, 16)
     g.wait_ge(S.lb, 16)
-    spread(T.sall, S.arrb)
-    g.sync.wait_ge(S.lb, 16)
-    g.sync.wait_ge(S.arrb, N - 1)
-    g.sync.dma_start(T.sall_sb[0:16, :], T.sall[:]).then_inc(S.lsb, 16)
-    g.tensor.wait_ge(S.fill, 2)
-    g.tensor.wait_ge(S.lsb, 16)
-    g.tensor.matmul(T.s_ps[:, 0:1], T.sall_sb[0:16, :], T.half[0:16, 0:1], True, True).then_inc(S.mm, 1)
-    g.vector.wait_ge(S.mm, 3)
-    g.vector.tensor_copy(T.sfin[:, 0:1], T.s_ps[:, 0:1]).then_inc(S.v, 1)
-    g.sync.wait_ge(S.v, 3)
-    g.sync.dma_start(T.s[:], T.sfin[:, 0:1]).then_inc(S.out, 16)
+    spread(T.sall[ci], peers, S.arrb)
+    g.wait_ge(S.arrb, len(peers))
+    g.remote_dma_fused([RemoteDMATransfer(
+        dst_ids=[_dst(topo, mate)], dma_engine_mask=eng[0], remote_sem=S.gots,
+        srcs=[T.sall[c] for c in range(nc)], dsts=[T.sres[:]], alu_op=1)], local_sem=S.sent)
+    g.sync.wait_ge(S.gots, 1)
+    g.sync.dma_start(T.s[:], T.sres[:]).then_inc(S.out, 16)
     g.sync.wait_ge(S.out, 32)
-    g.wait_ge(S.sent, 2 * len(eng))
+    g.wait_ge(S.sent, 3 * len(eng) + 1)

@@ -2,37 +2,52 @@ from concourse.bass import DstId, RemoteDMATransfer
 from concourse.mybir import AluOpType, AxisListType, ActivationFunctionType
 
 N = 16
-ENGINES = 4
+ROW_ENGINES = 4
+COL_ENGINES = 8
+STEP = 4
 
 SCRATCH = {
     "h_sb": ("sbuf", [128, 128], "bfloat16"),
-    "w_sb": ("sbuf", [128, 128], "bfloat16"),
-    "w2_sb": ("sbuf", [128, 128], "bfloat16"),
+    "w_all": ("sbuf", [128, 512], "bfloat16"),
     "zt_ps": ("psum", [128, 512], "float32"),
     "mt_ps": ("psum", [128, 512], "float32"),
     "mcol": ("sbuf", [128, 4], "float32"),
     "nb": ("sbuf", [128, 4], "float32"),
     "gm": ("sbuf", [128, 4], "float32"),
-    "scol": ("sbuf", [128, 4], "float32"),
-    "relu": ("sbuf", [128, 256], "float32"),
+    "stab": ("sbuf", [128, 4 * STEP], "float32"),
+    "sfin": ("sbuf", [128, 4], "float32"),
+    "relu": ("sbuf", [128, 512], "float32"),
     "half16": ("sbuf", [128, 16], "float32"),
     "ident": ("sbuf", [128, 16], "float32"),
     "mall_sb": ("sbuf", [128, 128], "float32"),
     "mall": ("dram", [N, 128, 1], "float32"),
-    "sall": ("dram", [N // 2, 128, 1], "float32"),
-    "sres": ("dram", [128, 1], "float32"),
 }
-SEMAPHORES = ["ldh", "ldw", "fill", "idn", "mm", "v", "vm", "sc", "la", "lb", "lma",
-              "arrw", "arra", "arrb", "gots", "out", "sent"]
+SEMAPHORES = ["ldh", "ldw", "fill", "idn", "mm", "mt", "mg", "v", "vm", "vs", "sc", "la", "lma",
+              "arrw", "arrg", "arra", "arrb", "out", "sent"]
 
 
-def _hops(topo, a, b):
-    ca, cb = topo.chip(a), topo.chip(b)
+def _chip_hops(topo, ca, cb):
     if ca == cb:
         return 0
     if topo.mates(ca, cb) or topo.same_plane(ca, cb):
         return 1
     return 2
+
+
+def _hops(topo, a, b):
+    return _chip_hops(topo, topo.chip(a), topo.chip(b))
+
+
+def _pairs(topo, chips):
+    if not chips:
+        return 0, []
+    a, best = chips[0], None
+    for b in chips[1:]:
+        c, m = _pairs(topo, [x for x in chips[1:] if x != b])
+        c += _chip_hops(topo, a, b)
+        if best is None or c < best[0]:
+            best = (c, [(a, b)] + m)
+    return best
 
 
 def _engines(topo, src, dsts, n):
@@ -63,22 +78,20 @@ def rank_program(g, core, T, topo):
     on_chip = {ch: sorted((c for c in T.cores if topo.chip(c) == ch), key=topo.die) for ch in chips}
     assert all(len(v) == 2 for v in on_chip.values())
     mine = on_chip[topo.chip(core)]
-    mate = mine[1 - mine.index(core)]
-    peers = sorted((on_chip[ch][mine.index(core)] for ch in chips if ch != topo.chip(core)), key=far_first)
-    ci = chips.index(topo.chip(core))
-    nc = len(chips)
-    eng = _engines(topo, core, others, ENGINES)
+    k = mine.index(core)
+    mate = mine[1 - k]
+    groups = [on_chip[a] + on_chip[b] for a, b in _pairs(topo, chips)[1]]
+    gi = [core in grp for grp in groups].index(True)
+    place = groups[gi].index(core)
+    paired = [c for c in groups[gi] if topo.chip(c) != topo.chip(core)]
+    peers = sorted((grp[place] for j, grp in enumerate(groups) if j != gi), key=far_first)
+    assert len(groups) * STEP == T.stab.shape[1]
+    col_eng = _engines(topo, core, others, COL_ENGINES)
+    row_eng = col_eng[:ROW_ENGINES]
+    blk = lambda j: slice(128 * j, 128 * (j + 1))
+    my_col = T.stab[:, STEP * gi:STEP * gi + 1]
 
-    def spread(slot, dsts, arr):
-        trs = []
-        for j, e in enumerate(eng):
-            part = dsts[j::len(eng)]
-            trs.append(RemoteDMATransfer(
-                dst_ids=[_dst(topo, d) for d in part], dma_engine_mask=e, remote_sem=arr,
-                srcs=[slot], dsts=[slot for _ in part], alu_op=0))
-        g.remote_dma_fused(trs, local_sem=S.sent)
-
-    g.scalar.dma_start(T.w_sb[:], T.w[:]).then_inc(S.ldw, 16)
+    g.scalar.dma_start(T.w_all[:, blk(0)], T.w[:]).then_inc(S.ldw, 16)
     g.sync.dma_start(T.h_sb[:], T.h[:]).then_inc(S.ldh, 16)
 
     g.vector.memset(T.half16[0:16, :], 0.5).then_inc(S.fill, 1)
@@ -87,50 +100,66 @@ def rank_program(g, core, T, topo):
 
     g.wait_ge(S.ldw, 16)
     rid, pid, _ = topo.addr(mate)
-    g.remote_dma(T.w2_sb[:], T.w_sb[:], S.arrw, S.sent, pid, rid, sum(eng))
+    g.remote_dma(T.w_all[:, blk(1)], T.w_all[:, blk(0)], S.arrw, S.sent, pid, rid, sum(row_eng))
 
     g.tensor.wait_ge(S.ldh, 16)
     g.tensor.wait_ge(S.ldw, 16)
-    g.tensor.matmul(T.zt_ps[:, 0:128], T.h_sb[:], T.w_sb[:], True, True).then_inc(S.mm, 1)
+    g.tensor.matmul(T.zt_ps[:, blk(0)], T.h_sb[:], T.w_all[:, blk(0)], True, True).then_inc(S.mm, 1)
     g.vector.wait_ge(S.mm, 1)
-    g.vector.tensor_reduce(T.mcol[:, 0:1], T.zt_ps[:, 0:128], AxisListType.X, AluOpType.max).then_inc(S.v, 1)
+    g.vector.tensor_reduce(T.mcol[:, 0:1], T.zt_ps[:, blk(0)], AxisListType.X, AluOpType.max).then_inc(S.v, 1)
 
     g.tensor.wait_ge(S.v, 1)
-    g.tensor.wait_ge(S.arrw, len(eng))
-    g.tensor.matmul(T.zt_ps[:, 128:256], T.h_sb[:], T.w2_sb[:], True, True).then_inc(S.mm, 1)
+    g.tensor.wait_ge(S.arrw, len(row_eng))
+    g.tensor.matmul(T.zt_ps[:, blk(1)], T.h_sb[:], T.w_all[:, blk(1)], True, True).then_inc(S.mm, 1)
 
     g.sync.wait_ge(S.v, 1)
     g.sync.dma_start(T.mall[rank], T.mcol[:, 0:1]).then_inc(S.la, 16)
     g.wait_ge(S.la, 16)
-    spread(T.mall[rank], others, S.arra)
+    trs = []
+    for j, e in enumerate(row_eng):
+        part = others[j::len(row_eng)]
+        trs.append(RemoteDMATransfer(
+            dst_ids=[_dst(topo, d) for d in part], dma_engine_mask=e, remote_sem=S.arra,
+            srcs=[T.mall[rank]], dsts=[T.mall[rank] for _ in part], alu_op=0))
+    g.remote_dma_fused(trs, local_sem=S.sent)
+
+    g.remote_dma_fused([RemoteDMATransfer(
+        dst_ids=[_dst(topo, d) for d in paired], dma_engine_mask=sum(col_eng), remote_sem=S.arrg,
+        srcs=[T.w_all[:, blk(0)]], dsts=[T.w_all[:, blk(2 + k)] for _ in paired], alu_op=0)], local_sem=S.sent)
+
     g.sync.wait_ge(S.la, 16)
     g.sync.wait_ge(S.arra, len(others))
     g.sync.dma_start(T.mall_sb[0:16, :], T.mall[:]).then_inc(S.lma, 16)
     g.tensor.wait_ge(S.idn, 1)
     g.tensor.wait_ge(S.lma, 16)
-    g.tensor.matmul(T.mt_ps[:, 0:16], T.mall_sb[0:16, :], T.ident[0:16, :], True, True).then_inc(S.mm, 1)
-    g.vector.wait_ge(S.mm, 3)
+    g.tensor.matmul(T.mt_ps[:, 0:16], T.mall_sb[0:16, :], T.ident[0:16, :], True, True).then_inc(S.mt, 1)
+    g.vector.wait_ge(S.mt, 1)
     g.vector.tensor_reduce(T.nb[:, 0:1], T.mt_ps[:, 0:16], AxisListType.X, AluOpType.max,
                            negate=True).then_inc(S.v, 1)
 
+    g.tensor.wait_ge(S.arrg, len(paired) * len(col_eng))
+    g.tensor.matmul(T.zt_ps[:, 256:512], T.h_sb[:], T.w_all[:, 256:512], True, True).then_inc(S.mg, 1)
+
     g.scalar.wait_ge(S.v, 2)
-    g.scalar.activation(T.relu[:], T.zt_ps[:, 0:256], ActivationFunctionType.Relu, bias=T.nb[:, 0:1], scale=1.0,
-                        accum_out=T.scol[:, 0:1]).then_inc(S.sc, 1)
+    g.scalar.wait_ge(S.mm, 2)
+    g.scalar.wait_ge(S.mg, 1)
+    g.scalar.activation(T.relu[:], T.zt_ps[:], ActivationFunctionType.Relu, bias=T.nb[:, 0:1], scale=1.0,
+                        accum_out=my_col).then_inc(S.sc, 1)
+
+    g.wait_ge(S.sc, 1)
+    g.remote_dma_fused([RemoteDMATransfer(
+        dst_ids=[_dst(topo, d) for d in peers], dma_engine_mask=sum(col_eng), remote_sem=S.arrb,
+        srcs=[my_col], dsts=[my_col for _ in peers], alu_op=0)], local_sem=S.sent)
 
     g.vector.wait_ge(S.v, 2)
     g.vector.tensor_scalar(T.gm[:, 0:1], T.nb[:, 0:1], -2.0, None, AluOpType.mult).then_inc(S.vm, 1)
     g.scalar.wait_ge(S.vm, 1)
     g.scalar.dma_start(T.m[:], T.gm[:, 0:1]).then_inc(S.out, 16)
 
-    g.sync.wait_ge(S.sc, 1)
-    g.sync.dma_start(T.sall[ci], T.scol[:, 0:1]).then_inc(S.lb, 16)
-    g.wait_ge(S.lb, 16)
-    spread(T.sall[ci], peers, S.arrb)
-    g.wait_ge(S.arrb, len(peers))
-    g.remote_dma_fused([RemoteDMATransfer(
-        dst_ids=[_dst(topo, mate)], dma_engine_mask=eng[0], remote_sem=S.gots,
-        srcs=[T.sall[c] for c in range(nc)], dsts=[T.sres[:]], alu_op=1)], local_sem=S.sent)
-    g.sync.wait_ge(S.gots, 1)
-    g.sync.dma_start(T.s[:], T.sres[:]).then_inc(S.out, 16)
+    g.vector.wait_ge(S.sc, 1)
+    g.vector.wait_ge(S.arrb, len(peers) * len(col_eng))
+    g.vector.tensor_reduce(T.sfin[:, 0:1], T.stab[:, 0:4 * STEP:STEP], AxisListType.X, AluOpType.add).then_inc(S.vs, 1)
+    g.sync.wait_ge(S.vs, 1)
+    g.sync.dma_start(T.s[:], T.sfin[:, 0:1]).then_inc(S.out, 16)
     g.sync.wait_ge(S.out, 32)
-    g.wait_ge(S.sent, 3 * len(eng) + 1)
+    g.wait_ge(S.sent, 2 * len(row_eng) + 2 * len(col_eng))

from concourse.bass import DstId, RemoteDMATransfer
from concourse.mybir import AluOpType, AxisListType, ActivationFunctionType

N = 16
ROW_ENGINES = 4
COL_ENGINES = 8
STEP = 4

SCRATCH = {
    "h_sb": ("sbuf", [128, 128], "bfloat16"),
    "w_all": ("sbuf", [128, 512], "bfloat16"),
    "zt_ps": ("psum", [128, 512], "float32"),
    "mt_ps": ("psum", [128, 512], "float32"),
    "mcol": ("sbuf", [128, 4], "float32"),
    "nb": ("sbuf", [128, 4], "float32"),
    "gm": ("sbuf", [128, 4], "float32"),
    "stab": ("sbuf", [128, 4 * STEP], "float32"),
    "sfin": ("sbuf", [128, 4], "float32"),
    "relu": ("sbuf", [128, 512], "float32"),
    "half16": ("sbuf", [128, 16], "float32"),
    "ident": ("sbuf", [128, 16], "float32"),
    "mall_sb": ("sbuf", [128, 128], "float32"),
    "mall": ("dram", [N, 128, 1], "float32"),
}
SEMAPHORES = ["ldh", "ldw", "fill", "idn", "mm", "mt", "mg", "v", "vm", "vs", "sc", "la", "lma",
              "arrw", "arrg", "arra", "arrb", "out", "sent"]


def _chip_hops(topo, ca, cb):
    if ca == cb:
        return 0
    if topo.mates(ca, cb) or topo.same_plane(ca, cb):
        return 1
    return 2


def _hops(topo, a, b):
    return _chip_hops(topo, topo.chip(a), topo.chip(b))


def _pairs(topo, chips):
    if not chips:
        return 0, []
    a, best = chips[0], None
    for b in chips[1:]:
        c, m = _pairs(topo, [x for x in chips[1:] if x != b])
        c += _chip_hops(topo, a, b)
        if best is None or c < best[0]:
            best = (c, [(a, b)] + m)
    return best


def _engines(topo, src, dsts, n):
    m = topo.mask(src, dsts[0])
    for d in dsts[1:]:
        m &= topo.mask(src, d)
    bits = [1 << b for b in range(m.bit_length()) if (m >> b) & 1]
    k = 1
    while k * 2 <= min(n, len(bits)):
        k *= 2
    return bits[:k]


def _dst(topo, c):
    rid, pid, _ = topo.addr(c)
    return DstId(rid=rid, pnc=pid)


def rank_program(g, core, T, topo):
    rank = T.rank_of(core)
    if rank is None:
        return
    S = T.sem
    far_first = lambda c: -_hops(topo, core, c)
    others = sorted((c for c in T.cores if c != core), key=far_first)
    assert all(topo.may_write(core, c) for c in others)
    chips = sorted({topo.chip(c) for c in T.cores})
    on_chip = {ch: sorted((c for c in T.cores if topo.chip(c) == ch), key=topo.die) for ch in chips}
    assert all(len(v) == 2 for v in on_chip.values())
    mine = on_chip[topo.chip(core)]
    k = mine.index(core)
    mate = mine[1 - k]
    groups = [on_chip[a] + on_chip[b] for a, b in _pairs(topo, chips)[1]]
    gi = [core in grp for grp in groups].index(True)
    place = groups[gi].index(core)
    paired = [c for c in groups[gi] if topo.chip(c) != topo.chip(core)]
    peers = sorted((grp[place] for j, grp in enumerate(groups) if j != gi), key=far_first)
    assert len(groups) * STEP == T.stab.shape[1]
    col_eng = _engines(topo, core, others, COL_ENGINES)
    row_eng = col_eng[:ROW_ENGINES]
    blk = lambda j: slice(128 * j, 128 * (j + 1))
    my_col = T.stab[:, STEP * gi:STEP * gi + 1]

    g.scalar.dma_start(T.w_all[:, blk(0)], T.w[:]).then_inc(S.ldw, 16)
    g.sync.dma_start(T.h_sb[:], T.h[:]).then_inc(S.ldh, 16)

    g.vector.memset(T.half16[0:16, :], 0.5).then_inc(S.fill, 1)
    g.wait_ge(S.fill, 1)
    g.affine_select(T.ident[0:16, :], T.half16[0:16, :], [[-1, 16]], AluOpType.is_equal, 0.0, 0, 1).then_inc(S.idn, 1)

    g.wait_ge(S.ldw, 16)
    rid, pid, _ = topo.addr(mate)
    g.remote_dma(T.w_all[:, blk(1)], T.w_all[:, blk(0)], S.arrw, S.sent, pid, rid, sum(row_eng))

    g.tensor.wait_ge(S.ldh, 16)
    g.tensor.wait_ge(S.ldw, 16)
    g.tensor.matmul(T.zt_ps[:, blk(0)], T.h_sb[:], T.w_all[:, blk(0)], True, True).then_inc(S.mm, 1)
    g.vector.wait_ge(S.mm, 1)
    g.vector.tensor_reduce(T.mcol[:, 0:1], T.zt_ps[:, blk(0)], AxisListType.X, AluOpType.max).then_inc(S.v, 1)

    g.tensor.wait_ge(S.v, 1)
    g.tensor.wait_ge(S.arrw, len(row_eng))
    g.tensor.matmul(T.zt_ps[:, blk(1)], T.h_sb[:], T.w_all[:, blk(1)], True, True).then_inc(S.mm, 1)

    g.sync.wait_ge(S.v, 1)
    g.sync.dma_start(T.mall[rank], T.mcol[:, 0:1]).then_inc(S.la, 16)
    g.wait_ge(S.la, 16)
    trs = []
    for j, e in enumerate(row_eng):
        part = others[j::len(row_eng)]
        trs.append(RemoteDMATransfer(
            dst_ids=[_dst(topo, d) for d in part], dma_engine_mask=e, remote_sem=S.arra,
            srcs=[T.mall[rank]], dsts=[T.mall[rank] for _ in part], alu_op=0))
    g.remote_dma_fused(trs, local_sem=S.sent)

    g.remote_dma_fused([RemoteDMATransfer(
        dst_ids=[_dst(topo, d) for d in paired], dma_engine_mask=sum(col_eng), remote_sem=S.arrg,
        srcs=[T.w_all[:, blk(0)]], dsts=[T.w_all[:, blk(2 + k)] for _ in paired], alu_op=0)], local_sem=S.sent)

    g.sync.wait_ge(S.la, 16)
    g.sync.wait_ge(S.arra, len(others))
    g.sync.dma_start(T.mall_sb[0:16, :], T.mall[:]).then_inc(S.lma, 16)
    g.tensor.wait_ge(S.idn, 1)
    g.tensor.wait_ge(S.lma, 16)
    g.tensor.matmul(T.mt_ps[:, 0:16], T.mall_sb[0:16, :], T.ident[0:16, :], True, True).then_inc(S.mt, 1)
    g.vector.wait_ge(S.mt, 1)
    g.vector.tensor_reduce(T.nb[:, 0:1], T.mt_ps[:, 0:16], AxisListType.X, AluOpType.max,
                           negate=True).then_inc(S.v, 1)

    g.tensor.wait_ge(S.arrg, len(paired) * len(col_eng))
    g.tensor.matmul(T.zt_ps[:, 256:512], T.h_sb[:], T.w_all[:, 256:512], True, True).then_inc(S.mg, 1)

    g.scalar.wait_ge(S.v, 2)
    g.scalar.wait_ge(S.mm, 2)
    g.scalar.wait_ge(S.mg, 1)
    g.scalar.activation(T.relu[:], T.zt_ps[:], ActivationFunctionType.Relu, bias=T.nb[:, 0:1], scale=1.0,
                        accum_out=my_col).then_inc(S.sc, 1)

    g.wait_ge(S.sc, 1)
    g.remote_dma_fused([RemoteDMATransfer(
        dst_ids=[_dst(topo, d) for d in peers], dma_engine_mask=sum(col_eng), remote_sem=S.arrb,
        srcs=[my_col], dsts=[my_col for _ in peers], alu_op=0)], local_sem=S.sent)

    g.vector.wait_ge(S.v, 2)
    g.vector.tensor_scalar(T.gm[:, 0:1], T.nb[:, 0:1], -2.0, None, AluOpType.mult).then_inc(S.vm, 1)
    g.scalar.wait_ge(S.vm, 1)
    g.scalar.dma_start(T.m[:], T.gm[:, 0:1]).then_inc(S.out, 16)

    g.vector.wait_ge(S.sc, 1)
    g.vector.wait_ge(S.arrb, len(peers) * len(col_eng))
    g.vector.tensor_reduce(T.sfin[:, 0:1], T.stab[:, 0:4 * STEP:STEP], AxisListType.X, AluOpType.add).then_inc(S.vs, 1)
    g.sync.wait_ge(S.vs, 1)
    g.sync.dma_start(T.s[:], T.sfin[:, 0:1]).then_inc(S.out, 16)
    g.sync.wait_ge(S.out, 32)
    g.wait_ge(S.sent, 2 * len(row_eng) + 2 * len(col_eng))
